import numpy as np
import ml_dtypes


def mxq(x, axis, fmt="e4m3"):
    dtype, down = {"e4m3": (ml_dtypes.float8_e4m3fn, 7), "e5m2": (ml_dtypes.float8_e5m2, 14)}[fmt]
    v = np.moveaxis(np.asarray(x, np.float32).astype(ml_dtypes.bfloat16).astype(np.float64), axis, -1)
    blocks = v.reshape(v.shape[:-1] + (-1, 32))
    amax = np.abs(blocks).max(-1, keepdims=True)
    byte = np.maximum(np.where(amax > 0, np.frexp(amax)[1] - 1 + 127, 0) - down, 1)
    scale = np.exp2(byte - 127.0)
    codes = (blocks / scale).astype(np.float32).astype(dtype).astype(np.float64)
    return np.moveaxis((codes * scale).reshape(v.shape), -1, axis)


WIDE = False


def mx_kscale(k):
    if not WIDE:
        return np.ones(k)
    levels = np.array([10, -10, 5, -5, 0])
    if k % 512:
        return np.exp2(np.random.permutation(np.resize(levels, k // 32))).repeat(32)
    a = np.empty((k // 512, 16))
    for p in range(k // 512):
        a[p, :8] = np.random.permutation(np.resize(levels, 8))
        for g in range(8):
            far = levels[np.abs(levels - a[p, g]) >= 10]
            a[p, g + 8] = far[np.random.randint(len(far))]
    return np.exp2(a.ravel()).repeat(32)


BF16 = ml_dtypes.bfloat16


def bf(x):
    return np.asarray(x, np.float32).astype(BF16)


def f64(x):
    return np.asarray(x).astype(np.float64)


E2M1 = np.array([0.0, 0.5, 1.0, 1.5, 2.0, 3.0, 4.0, 6.0, -0.0, -0.5, -1.0, -1.5, -2.0, -3.0, -4.0, -6.0])


def pack_weight(w, fmt):
    k, n = w.shape
    w = f64(bf(w)).reshape(k // 32, 32, n)
    amax = np.abs(w).max(1)
    if fmt == "e4m3":
        byte = np.frexp(amax)[1] - 1 + 127 - 7
    else:
        mant, ex = np.frexp(amax / 6.0)
        byte = np.where(mant > 0.5, ex, ex - 1) + 127
    byte = np.clip(np.where(amax > 0, byte, 1), 1, 254)
    scaled = (w * np.exp2(127.0 - byte)[:, None, :]).reshape(k, n).astype(np.float32)
    by_word = np.ascontiguousarray(scaled.reshape(k // 512, 128, 4, n).transpose(0, 1, 3, 2))
    if fmt == "e4m3":
        words = by_word.astype(ml_dtypes.float8_e4m3fn).view(np.uint8)
    else:
        c = by_word.astype(ml_dtypes.float4_e2m1fn).view(np.uint8) & 0xF
        words = c[..., 0::2] | (c[..., 1::2] << 4)
    return np.ascontiguousarray(words), np.ascontiguousarray(byte.astype(np.uint8).reshape(k // 512, 16, n))


def unpack_weight(words, scales, fmt):
    g, p, n, _ = words.shape
    if fmt == "e4m3":
        vals = np.ascontiguousarray(words).view(ml_dtypes.float8_e4m3fn).astype(np.float64)
    else:
        nib = np.empty((g, p, n, 4), np.uint8)
        nib[..., 0::2] = words & 0xF
        nib[..., 1::2] = words >> 4
        vals = E2M1[nib]
    vals = vals * np.repeat(np.exp2(scales.astype(np.float64) - 127.0), 8, axis=1)[..., None]
    return vals.transpose(0, 1, 3, 2).reshape(g * 512, n)
def pack4(w):
    words, scales = pack_weight(w, "e2m1")
    return words.reshape(words.shape[0], 128, -1), scales


def unpack4(words, scales):
    return unpack_weight(words.reshape(words.shape[0], 128, -1, 2), scales, "e2m1")


R, L, H, C = 2048, 1024, 1024, 512


def setup_inputs():
    s, t, u = mx_kscale(L), mx_kscale(L), mx_kscale(H)
    i = np.arange(L)
    side = np.where(i[:, None] <= i[None, :], 1.0, 0.5)
    length = np.random.uniform(0.5, 1.5, (L, L)) * side * 0.6 / np.sqrt(L)
    basis = np.random.standard_normal((H, L)) * u[:, None] / t
    mix = 0.3 * np.random.standard_normal((H, C)) / np.sqrt(H) / u[:, None]
    basis_words, basis_scales = pack4(basis)
    mix_words, mix_scales = pack4(mix)
    return {"dens": bf(np.random.standard_normal((R, L)) * s),
            "length": bf(length / s[:, None]),
            "opac": bf(np.random.uniform(0.1, 0.5, (R, L)) * t),
            "basis_words": basis_words, "basis_scales": basis_scales,
            "mix_words": mix_words, "mix_scales": mix_scales}


def reference(dens, length, opac, basis_words, basis_scales, mix_words, mix_scales):
    tau = mxq(f64(dens), 1, "e4m3") @ mxq(f64(length), 0, "e4m3")
    weight = np.exp(-tau) * f64(opac)
    basis = unpack4(basis_words, basis_scales)
    mix = unpack4(mix_words, mix_scales)
    func = basis.T @ mix
    return mxq(weight, 1, "e4m3") @ mxq(func, 0, "e4m3")

@@ -1,0 +1,325 @@
+from contextlib import ExitStack
+
+import concourse.mybir as mybir
+from concourse.masks import make_identity
+
+R, L, H, C = 2048, 1024, 1024, 512
+FLOPS = 2 * R * L * L + 2 * H * L * C + 2 * R * L * C
+
+F32 = mybir.dt.float32
+BF16 = mybir.dt.bfloat16
+I32 = mybir.dt.int32
+U32 = mybir.dt.uint32
+U8 = mybir.dt.uint8
+FP8X4 = mybir.dt.float8_e4m3fn_x4
+FP4X4 = mybir.dt.float4_e2m1fn_x4
+EXP = mybir.ActivationFunctionType.Exp
+
+P = 128
+KP = 512
+RAYS = 256
+CHUNKS = R // RAYS
+
+
+def tile_ray_depth_moments_s12_kernel(
+    tc, dens, length, opac, basis_words, basis_scales, mix_words, mix_scales, out
+):
+    nc = tc.nc
+    with ExitStack() as ctx:
+        keep = ctx.enter_context(tc.tile_pool(name="keep", bufs=1))
+        work = ctx.enter_context(tc.tile_pool(name="work", bufs=2))
+        psum = ctx.enter_context(tc.psum_pool(name="psum", bufs=4))
+        ctx.enter_context(tc.manual_schedule())
+
+        def kept(name, shape, dtype):
+            return keep.tile(shape, dtype, name=name, align_bytes=64)
+
+        def ring(tag, shape, dtype, bufs):
+            return work.tile(shape, dtype, name=tag, tag=tag, bufs=bufs, align_bytes=64)
+
+        def bank(tag):
+            return psum.tile([P, KP], F32, name=tag, tag=tag, bufs=4 if tag == "mm" else 2)
+
+        fp4_scales = kept("fp4_scales", [P, 2, L + C], U8)
+        nc.vector.memset(fp4_scales[:].rearrange("p g n -> p (g n)").bitcast(I32), 0)
+        warm = kept("warm", [P, 2], F32)
+        nc.vector.memset(warm[:], 0.0)
+        ident = kept("ident", [P, P], F32)
+        make_identity(nc, ident[:])
+        nc.scalar.activation(out=warm[:, 1:2], in_=warm[:, 0:1], func=EXP)
+
+        def load_scales(src, cols, q):
+            nc.sync.dma_start(
+                out=fp4_scales[32 * q : 32 * q + 4, :, cols].bitcast(I32),
+                in_=src[:, 4 * q : 4 * q + 4, :].rearrange("g r n -> r g n").bitcast(I32),
+            )
+
+        mix = kept("mix", [P, 2, 2 * C], U8)
+        basis = {}
+
+        def load_basis(s):
+            t = kept("basis%d" % s, [P, 2, 2 * KP], U8)
+            nc.sync.dma_start(
+                out=t[:].bitcast(I32),
+                in_=basis_words[:, :, 2 * KP * s : 2 * KP * (s + 1)].rearrange("g p n -> p g n").bitcast(I32),
+            )
+            basis[s] = t
+
+        len_raw = {}
+        rows_in = {}
+
+        def load_length(s, g):
+            t = kept("len_raw%d%d" % (s, g), [P, 4, KP], BF16)
+            nc.sync.dma_start(
+                out=t[:],
+                in_=length[KP * g : KP * (g + 1), KP * s : KP * (s + 1)].rearrange("(p j) n -> p j n", j=4),
+            )
+            len_raw[s, g] = t
+
+        def load_rows(which, src, i):
+            t = kept("%s%d" % (which, i), [P, 2 * L], BF16)
+            nc.sync.dma_start(
+                out=t[:], in_=src[RAYS * i : RAYS * (i + 1), :].rearrange("(p n) k -> p (n k)", n=2)
+            )
+            rows_in[which, i] = t
+
+        load_rows("dens", dens, 0)
+        for q in range(4):
+            load_scales(mix_scales, slice(L, L + C), q)
+        for q in range(2):
+            load_scales(basis_scales, slice(0, L), q)
+        nc.sync.dma_start(out=mix[:].bitcast(I32), in_=mix_words.rearrange("g p n -> p g n").bitcast(I32))
+        for q in range(2, 4):
+            load_scales(basis_scales, slice(0, L), q)
+        load_basis(0)
+        load_length(0, 0)
+        load_basis(1)
+        load_length(0, 1)
+        load_length(1, 0)
+        load_length(1, 1)
+        for i in range(CHUNKS):
+            load_rows("opac", opac, i)
+            if i + 1 < CHUNKS:
+                load_rows("dens", dens, i + 1)
+
+        len_grouped = {}
+        len_mx = {}
+        func_sorted = {}
+        func_grouped = {}
+        func_mx = {}
+        sorted_words = {}
+        turned = {}
+        dens_grouped = {}
+        dens_mx = {}
+        trans = {}
+        weight = {}
+        weight_mx = {}
+
+        def quantize(codes, scales, grouped):
+            nc.vector.quantize_mx(out=codes.bitcast(FP8X4), scales=scales, in_=grouped)
+
+        def length_interleave(s, g):
+            t = ring("len_grouped", [P, 4 * KP], BF16, 3)
+            nc.vector.tensor_copy(
+                out=t[:].rearrange("p (t a b j) -> p a t b j", t=4, b=2, j=4),
+                in_=len_raw[s, g][:].rearrange("p j (a b t) -> p a t b j", b=2, t=4),
+            )
+            len_grouped[s, g] = t
+
+        def length_quantize(s, g):
+            codes = kept("len_codes%d%d" % (s, g), [P, KP], U32)
+            scales = kept("len_scales%d%d" % (s, g), [P, KP], U8)
+            quantize(codes[:], scales[:], len_grouped[s, g][:])
+            len_mx[s, g] = (codes, scales)
+
+        def func_products(s):
+            t = kept("func_sorted%d" % s, [P, 4, KP], BF16)
+            for ct in range(4):
+                acc = bank("mm")
+                for g in range(2):
+                    nc.tensor.matmul_mx(
+                        out=acc[:],
+                        lhsT=mix[:, g, 2 * P * ct : 2 * P * (ct + 1)].bitcast(FP4X4),
+                        lhsT_scale=fp4_scales[:, g, L + P * ct : L + P * (ct + 1)],
+                        rhs=basis[s][:, g, :].bitcast(FP4X4),
+                        rhs_scale=fp4_scales[:, g, KP * s : KP * (s + 1)],
+                        start=(g == 0),
+                        stop=(g == 1),
+                    )
+                nc.scalar.copy(
+                    out=t[:, ct, :].rearrange("p (u m e) -> p u m e", u=2, e=2),
+                    in_=acc[:].rearrange("p (m u e) -> p u m e", u=2, e=2),
+                )
+            func_sorted[s] = t
+
+        def func_turn(s):
+            words = func_sorted[s][:].rearrange("p c n -> p (c n)").bitcast(F32)
+            t = kept("func_grouped%d" % s, [P, 4 * C], BF16)
+            for half in range(2):
+                acc = bank("mm")
+                for u in range(2):
+                    for c in range(2):
+                        w0 = 256 * (2 * half + c) + P * u
+                        o0 = 256 * u + P * c
+                        nc.tensor.transpose(acc[:, o0 : o0 + P], words[:, w0 : w0 + P], ident[:])
+                nc.scalar.copy(
+                    out=t[:].bitcast(F32)[:, KP * half : KP * (half + 1)].rearrange("p (n u) -> p n u", u=2),
+                    in_=acc[:].rearrange("p (u n) -> p n u", u=2),
+                )
+            func_grouped[s] = t
+
+        def func_quantize(s):
+            codes = kept("func_codes%d" % s, [P, C], U32)
+            scales = kept("func_scales%d" % s, [P, C], U8)
+            quantize(codes[:], scales[:], func_grouped[s][:])
+            func_mx[s] = (codes, scales)
+
+        def sort_words(which, i):
+            t = ring(which + "_sorted", [P, 2, KP], F32, 2)
+            nc.vector.tensor_copy(
+                out=t[:].rearrange("p u (a b) -> p a u b", b=4),
+                in_=rows_in[which, i][:].bitcast(F32).rearrange("p (a b u) -> p a u b", b=4, u=2),
+            )
+            sorted_words[which, i] = t
+
+        def turn_rows(which, i):
+            for g in range(2):
+                acc = bank(which)
+                for u in range(2):
+                    for n in range(2):
+                        if (which, i) in sorted_words:
+                            w0 = 256 * n + P * g
+                            src = sorted_words[which, i][:, u, w0 : w0 + P]
+                        else:
+                            w0 = KP * n + 256 * g
+                            src = rows_in[which, i][:].bitcast(F32)[:, w0 + u : w0 + 256 : 2]
+                        o0 = 256 * u + P * n
+                        nc.tensor.transpose(acc[:, o0 : o0 + P], src, ident[:])
+                turned[which, i, g] = acc
+
+        def dens_copy(i):
+            t = ring("dens_grouped", [P, 2 * 4 * RAYS], BF16, 2)
+            for g in range(2):
+                nc.scalar.copy(
+                    out=t[:].bitcast(F32)[:, KP * g : KP * (g + 1)].rearrange("p (r u) -> p r u", u=2),
+                    in_=turned["dens", i, g][:].rearrange("p (u r) -> p r u", u=2),
+                )
+            dens_grouped[i] = t
+
+        def dens_quantize(i):
+            codes = ring("dens_codes", [P, 2 * RAYS], U32, 2)
+            scales = ring("dens_scales", [P, 2 * RAYS], U8, 2)
+            quantize(codes[:], scales[:], dens_grouped[i][:])
+            dens_mx[i] = (codes, scales)
+
+        def depth_and_exp(i, s):
+            t = ring("trans", [P, 2, 2 * RAYS], F32, 3)
+            d_codes, d_scales = dens_mx[i]
+            for u in range(2):
+                acc = bank("mm")
+                for e in range(2):
+                    cols = slice(P * (2 * u + e), P * (2 * u + e + 1))
+                    for g in range(2):
+                        l_codes, l_scales = len_mx[s, g]
+                        rays = slice(RAYS * g, RAYS * (g + 1))
+                        nc.tensor.matmul_mx(
+                            out=acc[:, RAYS * e : RAYS * (e + 1)],
+                            lhsT=l_codes[:, cols].bitcast(FP8X4),
+                            lhsT_scale=l_scales[:, cols],
+                            rhs=d_codes[:, rays].bitcast(FP8X4),
+                            rhs_scale=d_scales[:, rays],
+                            start=(g == 0),
+                            stop=(g == 1),
+                        )
+                nc.scalar.activation(
+                    out=t[:, u, :].rearrange("p (r e) -> p r e", e=2),
+                    in_=acc[:].rearrange("p (e r) -> p r e", e=2),
+                    func=EXP,
+                    scale=-1.0,
+                )
+            trans[i, s] = t
+
+        def weigh(i, s):
+            if s == 0:
+                weight[i] = ring("weight", [P, 2 * 4 * RAYS], BF16, 2)
+            nc.vector.tensor_tensor(
+                out=weight[i][:, 4 * RAYS * s : 4 * RAYS * (s + 1)].rearrange("p (r u e) -> p r u e", u=2, e=2),
+                in0=trans[i, s][:].rearrange("p u (r e) -> p r u e", e=2),
+                in1=turned["opac", i, s][:].bitcast(BF16).rearrange("p (u r e) -> p r u e", u=2, e=2),
+                op=mybir.AluOpType.mult,
+            )
+
+        def weight_quantize(i):
+            codes = ring("weight_codes", [P, 2 * RAYS], U32, 2)
+            scales = ring("weight_scales", [P, 2 * RAYS], U8, 2)
+            quantize(codes[:], scales[:], weight[i][:])
+            weight_mx[i] = (codes, scales)
+
+        def moments(i):
+            w_codes, w_scales = weight_mx[i]
+            t = ring("result", [P, 2 * C], F32, 4)
+            for n in range(2):
+                acc = bank("mm")
+                for s in range(2):
+                    f_codes, f_scales = func_mx[s]
+                    rays = slice(RAYS * s + P * n, RAYS * s + P * (n + 1))
+                    nc.tensor.matmul_mx(
+                        out=acc[:],
+                        lhsT=w_codes[:, rays].bitcast(FP8X4),
+                        lhsT_scale=w_scales[:, rays],
+                        rhs=f_codes[:].bitcast(FP8X4),
+                        rhs_scale=f_scales[:],
+                        start=(s == 0),
+                        stop=(s == 1),
+                    )
+                nc.scalar.copy(out=t[:, C * n : C * (n + 1)], in_=acc[:])
+            nc.sync.dma_start(
+                out=out[RAYS * i : RAYS * (i + 1), :].rearrange("(p n) c -> p (n c)", n=2), in_=t[:]
+            )
+
+        turn_rows("dens", 0)
+        dens_copy(0)
+        func_products(0)
+        func_products(1)
+        length_interleave(0, 0)
+        dens_quantize(0)
+        length_quantize(0, 0)
+        length_interleave(0, 1)
+        length_interleave(1, 0)
+        length_quantize(0, 1)
+        length_quantize(1, 0)
+        length_interleave(1, 1)
+        length_quantize(1, 1)
+        depth_and_exp(0, 0)
+        turn_rows("opac", 0)
+        turn_rows("dens", 1)
+        dens_copy(1)
+        weigh(0, 0)
+        dens_quantize(1)
+        sort_words("dens", 2)
+        sort_words("opac", 1)
+        depth_and_exp(0, 1)
+        weigh(0, 1)
+        func_turn(0)
+        func_turn(1)
+
+        for i in range(1, CHUNKS):
+            if i + 2 < CHUNKS:
+                sort_words("dens", i + 2)
+            weight_quantize(i - 1)
+            if i + 1 < CHUNKS:
+                turn_rows("dens", i + 1)
+            turn_rows("opac", i)
+            if i == 1:
+                func_quantize(0)
+                func_quantize(1)
+            if i + 1 < CHUNKS:
+                dens_copy(i + 1)
+                dens_quantize(i + 1)
+                sort_words("opac", i + 1)
+            for s in range(2):
+                depth_and_exp(i, s)
+                weigh(i, s)
+            moments(i - 1)
+        weight_quantize(CHUNKS - 1)
+        moments(CHUNKS - 1)

@@ -84,23 +84,23 @@ def tile_ray_depth_moments_s12_kernel(
             rows_in[which, i] = t
 
         load_rows("dens", dens, 0)
+        load_rows("opac", opac, 0)
         for q in range(4):
             load_scales(mix_scales, slice(L, L + C), q)
-        for q in range(2):
-            load_scales(basis_scales, slice(0, L), q)
+        load_rows("dens", dens, 1)
         nc.sync.dma_start(out=mix[:].bitcast(I32), in_=mix_words.rearrange("g p n -> p g n").bitcast(I32))
-        for q in range(2, 4):
-            load_scales(basis_scales, slice(0, L), q)
         load_basis(0)
-        load_length(0, 0)
+        for q in range(4):
+            load_scales(basis_scales, slice(0, L), q)
         load_basis(1)
+        load_length(0, 0)
         load_length(0, 1)
         load_length(1, 0)
         load_length(1, 1)
-        for i in range(CHUNKS):
-            load_rows("opac", opac, i)
-            if i + 1 < CHUNKS:
-                load_rows("dens", dens, i + 1)
+        for i in range(2, CHUNKS):
+            load_rows("opac", opac, i - 1)
+            load_rows("dens", dens, i)
+        load_rows("opac", opac, CHUNKS - 1)
 
         len_grouped = {}
         len_mx = {}
@@ -213,7 +213,7 @@ def tile_ray_depth_moments_s12_kernel(
             dens_mx[i] = (codes, scales)
 
         def depth_and_exp(i, s):
-            t = ring("trans", [P, 2, 2 * RAYS], F32, 3)
+            t = ring("trans", [P, 2, 2 * RAYS], F32, 4)
             d_codes, d_scales = dens_mx[i]
             for u in range(2):
                 acc = bank("mm")
@@ -249,6 +249,62 @@ def tile_ray_depth_moments_s12_kernel(
                 op=mybir.AluOpType.mult,
             )
 
+        def depth_and_exp_tile(i, s, n):
+            t = ring("trans", [P, 4 * P], F32, 4)
+            d_codes, d_scales = dens_mx[i]
+            acc = bank("mm")
+            for slot in range(4):
+                cols = slice(P * slot, P * (slot + 1))
+                for g in range(2):
+                    l_codes, l_scales = len_mx[s, g]
+                    rays = slice(RAYS * g + P * n, RAYS * g + P * (n + 1))
+                    nc.tensor.matmul_mx(
+                        out=acc[:, cols],
+                        lhsT=l_codes[:, cols].bitcast(FP8X4),
+                        lhsT_scale=l_scales[:, cols],
+                        rhs=d_codes[:, rays].bitcast(FP8X4),
+                        rhs_scale=d_scales[:, rays],
+                        start=(g == 0),
+                        stop=(g == 1),
+                    )
+            nc.scalar.activation(
+                out=t[:].rearrange("p (r t) -> p r t", t=4),
+                in_=acc[:].rearrange("p (t r) -> p r t", t=4),
+                func=EXP,
+                scale=-1.0,
+            )
+            trans[i, s, n] = t
+
+        def weigh_tile(i, s, n):
+            t = ring("weight_tile", [P, 4 * P], BF16, 2)
+            nc.vector.tensor_tensor(
+                out=t[:].rearrange("p (r u e) -> p r u e", u=2, e=2),
+                in0=trans[i, s, n][:].rearrange("p (r u e) -> p r u e", u=2, e=2),
+                in1=turned["opac", i, s][:]
+                .bitcast(BF16)
+                .rearrange("p (u r e) -> p r u e", u=2, e=2)[:, P * n : P * (n + 1)],
+                op=mybir.AluOpType.mult,
+            )
+            weight[i, s, n] = t
+
+        def quantize_part(name, grouped, width):
+            codes = kept(name + "_codes", [P, width], U32)
+            scales = kept(name + "_scales", [P, width], U8)
+            quantize(codes[:], scales[:], grouped)
+            return codes, scales
+
+        def moments_pass(acc, w_mx, rays, s):
+            f_codes, f_scales = func_mx[s]
+            nc.tensor.matmul_mx(
+                out=acc[:],
+                lhsT=w_mx[0][:, rays].bitcast(FP8X4),
+                lhsT_scale=w_mx[1][:, rays],
+                rhs=f_codes[:].bitcast(FP8X4),
+                rhs_scale=f_scales[:],
+                start=(s == 0),
+                stop=(s == 1),
+            )
+
         def weight_quantize(i):
             codes = ring("weight_codes", [P, 2 * RAYS], U32, 2)
             scales = ring("weight_scales", [P, 2 * RAYS], U8, 2)
@@ -278,48 +334,71 @@ def tile_ray_depth_moments_s12_kernel(
             )
 
         turn_rows("dens", 0)
+        sort_words("opac", 0)
+        turn_rows("opac", 0)
         dens_copy(0)
+        sort_words("dens", 1)
+        dens_quantize(0)
+        turn_rows("dens", 1)
+        dens_copy(1)
+        dens_quantize(1)
         func_products(0)
         func_products(1)
         length_interleave(0, 0)
-        dens_quantize(0)
-        length_quantize(0, 0)
         length_interleave(0, 1)
-        length_interleave(1, 0)
+        length_quantize(0, 0)
         length_quantize(0, 1)
-        length_quantize(1, 0)
+        length_interleave(1, 0)
         length_interleave(1, 1)
+        length_quantize(1, 0)
         length_quantize(1, 1)
         depth_and_exp(0, 0)
-        turn_rows("opac", 0)
-        turn_rows("dens", 1)
-        dens_copy(1)
-        weigh(0, 0)
-        dens_quantize(1)
-        sort_words("dens", 2)
-        sort_words("opac", 1)
-        depth_and_exp(0, 1)
-        weigh(0, 1)
         func_turn(0)
         func_turn(1)
+        weigh(0, 0)
+        sort_words("dens", 2)
+        sort_words("opac", 1)
+        func_quantize(0)
+        depth_and_exp(0, 1)
+        weigh(0, 1)
+        func_quantize(1)
+        weight_quantize(0)
 
-        for i in range(1, CHUNKS):
+
+        last = CHUNKS - 1
+        for i in range(1, last):
+            depth_and_exp(i, 0)
+            turn_rows("dens", i + 1)
+            turn_rows("opac", i)
+            dens_copy(i + 1)
+            weigh(i, 0)
+            dens_quantize(i + 1)
             if i + 2 < CHUNKS:
                 sort_words("dens", i + 2)
-            weight_quantize(i - 1)
-            if i + 1 < CHUNKS:
-                turn_rows("dens", i + 1)
-            turn_rows("opac", i)
-            if i == 1:
-                func_quantize(0)
-                func_quantize(1)
-            if i + 1 < CHUNKS:
-                dens_copy(i + 1)
-                dens_quantize(i + 1)
-                sort_words("opac", i + 1)
-            for s in range(2):
-                depth_and_exp(i, s)
-                weigh(i, s)
+            depth_and_exp(i, 1)
+            weigh(i, 1)
+            if i + 2 < CHUNKS:
+                sort_words("opac", i + 2)
             moments(i - 1)
-        weight_quantize(CHUNKS - 1)
-        moments(CHUNKS - 1)
+            weight_quantize(i)
+
+        depth_and_exp(last, 0)
+        turn_rows("opac", last)
+        weigh(last, 0)
+        near = quantize_part("near", weight[last][:, : 4 * RAYS], RAYS)
+        for n in range(2):
+            depth_and_exp_tile(last, 1, n)
+            weigh_tile(last, 1, n)
+        far = [quantize_part("far%d" % n, weight[last, 1, n][:], P) for n in range(2)]
+        moments(last - 1)
+        accs = [bank("dens") for n in range(2)]
+        for n in range(2):
+            moments_pass(accs[n], near, slice(P * n, P * (n + 1)), 0)
+        for n in range(2):
+            moments_pass(accs[n], far[n], slice(0, P), 1)
+        for n, copy in enumerate((nc.scalar.copy, nc.vector.tensor_copy)):
+            t = ring("result", [P, C], F32, 4)
+            copy(out=t[:], in_=accs[n][:])
+            nc.sync.dma_start(
+                out=out[RAYS * last :, :].rearrange("(p n) c -> p n c", n=2)[:, n, :], in_=t[:]
+            )

@@ -42,11 +42,8 @@ def tile_ray_depth_moments_s12_kernel(
 
         fp4_scales = kept("fp4_scales", [P, 2, L + C], U8)
         nc.vector.memset(fp4_scales[:].rearrange("p g n -> p (g n)").bitcast(I32), 0)
-        warm = kept("warm", [P, 2], F32)
-        nc.vector.memset(warm[:], 0.0)
         ident = kept("ident", [P, P], F32)
         make_identity(nc, ident[:])
-        nc.scalar.activation(out=warm[:, 1:2], in_=warm[:, 0:1], func=EXP)
 
         def load_scales(src, cols, q):
             nc.sync.dma_start(
@@ -84,18 +81,18 @@ def tile_ray_depth_moments_s12_kernel(
             rows_in[which, i] = t
 
         load_rows("dens", dens, 0)
-        load_rows("opac", opac, 0)
         for q in range(4):
             load_scales(mix_scales, slice(L, L + C), q)
-        load_rows("dens", dens, 1)
+        load_length(0, 0)
+        load_rows("opac", opac, 0)
         nc.sync.dma_start(out=mix[:].bitcast(I32), in_=mix_words.rearrange("g p n -> p g n").bitcast(I32))
-        load_basis(0)
         for q in range(4):
             load_scales(basis_scales, slice(0, L), q)
-        load_basis(1)
-        load_length(0, 0)
+        load_basis(0)
         load_length(0, 1)
+        load_basis(1)
         load_length(1, 0)
+        load_rows("dens", dens, 1)
         load_length(1, 1)
         for i in range(2, CHUNKS):
             load_rows("opac", opac, i - 1)
@@ -152,7 +149,7 @@ def tile_ray_depth_moments_s12_kernel(
                 )
             func_sorted[s] = t
 
-        def func_turn(s):
+        def func_turn(s, copies):
             words = func_sorted[s][:].rearrange("p c n -> p (c n)").bitcast(F32)
             t = kept("func_grouped%d" % s, [P, 4 * C], BF16)
             for half in range(2):
@@ -162,7 +159,7 @@ def tile_ray_depth_moments_s12_kernel(
                         w0 = 256 * (2 * half + c) + P * u
                         o0 = 256 * u + P * c
                         nc.tensor.transpose(acc[:, o0 : o0 + P], words[:, w0 : w0 + P], ident[:])
-                nc.scalar.copy(
+                copies[half](
                     out=t[:].bitcast(F32)[:, KP * half : KP * (half + 1)].rearrange("p (n u) -> p n u", u=2),
                     in_=acc[:].rearrange("p (u n) -> p n u", u=2),
                 )
@@ -293,14 +290,14 @@ def tile_ray_depth_moments_s12_kernel(
             quantize(codes[:], scales[:], grouped)
             return codes, scales
 
-        def moments_pass(acc, w_mx, rays, s):
+        def moments_pass(acc, w_mx, rays, s, cols):
             f_codes, f_scales = func_mx[s]
             nc.tensor.matmul_mx(
-                out=acc[:],
+                out=acc[:, : C // 2],
                 lhsT=w_mx[0][:, rays].bitcast(FP8X4),
                 lhsT_scale=w_mx[1][:, rays],
-                rhs=f_codes[:].bitcast(FP8X4),
-                rhs_scale=f_scales[:],
+                rhs=f_codes[:, cols].bitcast(FP8X4),
+                rhs_scale=f_scales[:, cols],
                 start=(s == 0),
                 stop=(s == 1),
             )
@@ -334,32 +331,31 @@ def tile_ray_depth_moments_s12_kernel(
             )
 
         turn_rows("dens", 0)
-        sort_words("opac", 0)
         turn_rows("opac", 0)
         dens_copy(0)
-        sort_words("dens", 1)
+        length_interleave(0, 0)
         dens_quantize(0)
-        turn_rows("dens", 1)
-        dens_copy(1)
-        dens_quantize(1)
+        length_quantize(0, 0)
         func_products(0)
         func_products(1)
-        length_interleave(0, 0)
         length_interleave(0, 1)
-        length_quantize(0, 0)
-        length_quantize(0, 1)
         length_interleave(1, 0)
+        length_quantize(0, 1)
+        sort_words("dens", 1)
         length_interleave(1, 1)
         length_quantize(1, 0)
         length_quantize(1, 1)
         depth_and_exp(0, 0)
-        func_turn(0)
-        func_turn(1)
+        turn_rows("dens", 1)
+        dens_copy(1)
+        func_turn(0, (nc.scalar.copy, nc.scalar.copy))
         weigh(0, 0)
+        dens_quantize(1)
         sort_words("dens", 2)
         sort_words("opac", 1)
-        func_quantize(0)
         depth_and_exp(0, 1)
+        func_turn(1, (nc.scalar.copy, nc.scalar.copy))
+        func_quantize(0)
         weigh(0, 1)
         func_quantize(1)
         weight_quantize(0)
@@ -391,14 +387,17 @@ def tile_ray_depth_moments_s12_kernel(
             weigh_tile(last, 1, n)
         far = [quantize_part("far%d" % n, weight[last, 1, n][:], P) for n in range(2)]
         moments(last - 1)
-        accs = [bank("dens") for n in range(2)]
+        halves = [slice(0, C // 2), slice(C // 2, C)]
+        accs = [[bank("dens"), bank("dens")], [bank("mm"), bank("mm")]]
         for n in range(2):
-            moments_pass(accs[n], near, slice(P * n, P * (n + 1)), 0)
+            for h in range(2):
+                moments_pass(accs[n][h], near, slice(P * n, P * (n + 1)), 0, halves[h])
         for n in range(2):
-            moments_pass(accs[n], far[n], slice(0, P), 1)
-        for n, copy in enumerate((nc.scalar.copy, nc.vector.tensor_copy)):
+            for h in range(2):
+                moments_pass(accs[n][h], far[n], slice(0, P), 1, halves[h])
+        rows = out[RAYS * last :, :].rearrange("(p n) c -> p n c", n=2)
+        for n in range(2):
             t = ring("result", [P, C], F32, 4)
-            copy(out=t[:], in_=accs[n][:])
-            nc.sync.dma_start(
-                out=out[RAYS * last :, :].rearrange("(p n) c -> p n c", n=2)[:, n, :], in_=t[:]
-            )
+            nc.scalar.copy(out=t[:, halves[0]], in_=accs[n][0][:, : C // 2])
+            nc.vector.tensor_copy(out=t[:, halves[1]], in_=accs[n][1][:, : C // 2])
+            nc.sync.dma_start(out=rows[:, n, :], in_=t[:])

@@ -17,8 +17,11 @@ EXP = mybir.ActivationFunctionType.Exp
 
 P = 128
 KP = 512
+WORDS = KP // 2
+BANK = 512
 RAYS = 256
 CHUNKS = R // RAYS
+BANKS = {"mm": 4, "dens": 2, "opac": 2}
 
 
 def tile_ray_depth_moments_s12_kernel(
@@ -38,21 +41,26 @@ def tile_ray_depth_moments_s12_kernel(
             return work.tile(shape, dtype, name=tag, tag=tag, bufs=bufs, align_bytes=64)
 
         def bank(tag):
-            return psum.tile([P, KP], F32, name=tag, tag=tag, bufs=4 if tag == "mm" else 2)
+            return psum.tile([P, BANK], F32, name=tag, tag=tag, bufs=BANKS[tag])
 
-        fp4_scales = kept("fp4_scales", [P, 2, L + C], U8)
-        nc.vector.memset(fp4_scales[:].rearrange("p g n -> p (g n)").bitcast(I32), 0)
+        mix_plane = kept("mix_plane", [P, 2, C], U8)
+        basis_plane = kept("basis_plane", [P, 2, L], U8)
+        nc.gpsimd.memset(mix_plane[:].rearrange("p g n -> p (g n)").bitcast(I32), 0)
+        nc.vector.memset(basis_plane[:].rearrange("p g n -> p (g n)").bitcast(I32), 0)
         ident = kept("ident", [P, P], F32)
         make_identity(nc, ident[:])
 
-        def load_scales(src, cols, q):
-            nc.sync.dma_start(
-                out=fp4_scales[32 * q : 32 * q + 4, :, cols].bitcast(I32),
-                in_=src[:, 4 * q : 4 * q + 4, :].rearrange("g r n -> r g n").bitcast(I32),
-            )
-
         mix = kept("mix", [P, 2, 2 * C], U8)
         basis = {}
+        len_raw = {}
+        rows_in = {}
+
+        def load_scales(plane, src):
+            for q in range(4):
+                nc.sync.dma_start(
+                    out=plane[32 * q : 32 * q + 4].bitcast(I32),
+                    in_=src[:, 4 * q : 4 * q + 4, :].rearrange("g r n -> r g n").bitcast(I32),
+                )
 
         def load_basis(s):
             t = kept("basis%d" % s, [P, 2, 2 * KP], U8)
@@ -61,9 +69,6 @@ def tile_ray_depth_moments_s12_kernel(
                 in_=basis_words[:, :, 2 * KP * s : 2 * KP * (s + 1)].rearrange("g p n -> p g n").bitcast(I32),
             )
             basis[s] = t
-
-        len_raw = {}
-        rows_in = {}
 
         def load_length(s, g):
             t = kept("len_raw%d%d" % (s, g), [P, 4, KP], BF16)
@@ -81,13 +86,11 @@ def tile_ray_depth_moments_s12_kernel(
             rows_in[which, i] = t
 
         load_rows("dens", dens, 0)
-        for q in range(4):
-            load_scales(mix_scales, slice(L, L + C), q)
+        load_scales(mix_plane, mix_scales)
         load_length(0, 0)
         load_rows("opac", opac, 0)
         nc.sync.dma_start(out=mix[:].bitcast(I32), in_=mix_words.rearrange("g p n -> p g n").bitcast(I32))
-        for q in range(4):
-            load_scales(basis_scales, slice(0, L), q)
+        load_scales(basis_plane, basis_scales)
         load_basis(0)
         load_length(0, 1)
         load_basis(1)
@@ -113,7 +116,27 @@ def tile_ray_depth_moments_s12_kernel(
         weight_mx = {}
 
         def quantize(codes, scales, grouped):
-            nc.vector.quantize_mx(out=codes.bitcast(FP8X4), scales=scales, in_=grouped)
+            nc.vector.quantize_mx(out=codes[:].bitcast(FP8X4), scales=scales[:], in_=grouped)
+            return codes, scales
+
+        def quantize_kept(name, grouped, width):
+            return quantize(kept(name + "_codes", [P, width], U32), kept(name + "_scales", [P, width], U8), grouped)
+
+        def quantize_chunk(name, grouped):
+            return quantize(
+                ring(name + "_codes", [P, 2 * RAYS], U32, 2), ring(name + "_scales", [P, 2 * RAYS], U8, 2), grouped
+            )
+
+        def mx_pass(acc, stationary, s_cols, moving, m_cols, g):
+            nc.tensor.matmul_mx(
+                out=acc,
+                lhsT=stationary[0][:, s_cols].bitcast(FP8X4),
+                lhsT_scale=stationary[1][:, s_cols],
+                rhs=moving[0][:, m_cols].bitcast(FP8X4),
+                rhs_scale=moving[1][:, m_cols],
+                start=(g == 0),
+                stop=(g == 1),
+            )
 
         def length_interleave(s, g):
             t = ring("len_grouped", [P, 4 * KP], BF16, 3)
@@ -124,10 +147,7 @@ def tile_ray_depth_moments_s12_kernel(
             len_grouped[s, g] = t
 
         def length_quantize(s, g):
-            codes = kept("len_codes%d%d" % (s, g), [P, KP], U32)
-            scales = kept("len_scales%d%d" % (s, g), [P, KP], U8)
-            quantize(codes[:], scales[:], len_grouped[s, g][:])
-            len_mx[s, g] = (codes, scales)
+            len_mx[s, g] = quantize_kept("len%d%d" % (s, g), len_grouped[s, g][:], KP)
 
         def func_products(s):
             t = kept("func_sorted%d" % s, [P, 4, KP], BF16)
@@ -137,9 +157,9 @@ def tile_ray_depth_moments_s12_kernel(
                     nc.tensor.matmul_mx(
                         out=acc[:],
                         lhsT=mix[:, g, 2 * P * ct : 2 * P * (ct + 1)].bitcast(FP4X4),
-                        lhsT_scale=fp4_scales[:, g, L + P * ct : L + P * (ct + 1)],
+                        lhsT_scale=mix_plane[:, g, P * ct : P * (ct + 1)],
                         rhs=basis[s][:, g, :].bitcast(FP4X4),
-                        rhs_scale=fp4_scales[:, g, KP * s : KP * (s + 1)],
+                        rhs_scale=basis_plane[:, g, KP * s : KP * (s + 1)],
                         start=(g == 0),
                         stop=(g == 1),
                     )
@@ -149,30 +169,27 @@ def tile_ray_depth_moments_s12_kernel(
                 )
             func_sorted[s] = t
 
-        def func_turn(s, copies):
+        def func_turn(s):
             words = func_sorted[s][:].rearrange("p c n -> p (c n)").bitcast(F32)
             t = kept("func_grouped%d" % s, [P, 4 * C], BF16)
             for half in range(2):
                 acc = bank("mm")
                 for u in range(2):
                     for c in range(2):
-                        w0 = 256 * (2 * half + c) + P * u
-                        o0 = 256 * u + P * c
+                        w0 = WORDS * (2 * half + c) + P * u
+                        o0 = 2 * P * u + P * c
                         nc.tensor.transpose(acc[:, o0 : o0 + P], words[:, w0 : w0 + P], ident[:])
-                copies[half](
-                    out=t[:].bitcast(F32)[:, KP * half : KP * (half + 1)].rearrange("p (n u) -> p n u", u=2),
+                nc.scalar.copy(
+                    out=t[:].bitcast(F32)[:, BANK * half : BANK * (half + 1)].rearrange("p (n u) -> p n u", u=2),
                     in_=acc[:].rearrange("p (u n) -> p n u", u=2),
                 )
             func_grouped[s] = t
 
         def func_quantize(s):
-            codes = kept("func_codes%d" % s, [P, C], U32)
-            scales = kept("func_scales%d" % s, [P, C], U8)
-            quantize(codes[:], scales[:], func_grouped[s][:])
-            func_mx[s] = (codes, scales)
+            func_mx[s] = quantize_kept("func%d" % s, func_grouped[s][:], C)
 
         def sort_words(which, i):
-            t = ring(which + "_sorted", [P, 2, KP], F32, 2)
+            t = ring(which + "_sorted", [P, 2, 2 * WORDS], F32, 2)
             nc.vector.tensor_copy(
                 out=t[:].rearrange("p u (a b) -> p a u b", b=4),
                 in_=rows_in[which, i][:].bitcast(F32).rearrange("p (a b u) -> p a u b", b=4, u=2),
@@ -185,12 +202,12 @@ def tile_ray_depth_moments_s12_kernel(
                 for u in range(2):
                     for n in range(2):
                         if (which, i) in sorted_words:
-                            w0 = 256 * n + P * g
+                            w0 = WORDS * n + P * g
                             src = sorted_words[which, i][:, u, w0 : w0 + P]
                         else:
-                            w0 = KP * n + 256 * g
-                            src = rows_in[which, i][:].bitcast(F32)[:, w0 + u : w0 + 256 : 2]
-                        o0 = 256 * u + P * n
+                            w0 = 2 * WORDS * n + WORDS * g
+                            src = rows_in[which, i][:].bitcast(F32)[:, w0 + u : w0 + WORDS : 2]
+                        o0 = RAYS * u + P * n
                         nc.tensor.transpose(acc[:, o0 : o0 + P], src, ident[:])
                 turned[which, i, g] = acc
 
@@ -198,36 +215,23 @@ def tile_ray_depth_moments_s12_kernel(
             t = ring("dens_grouped", [P, 2 * 4 * RAYS], BF16, 2)
             for g in range(2):
                 nc.scalar.copy(
-                    out=t[:].bitcast(F32)[:, KP * g : KP * (g + 1)].rearrange("p (r u) -> p r u", u=2),
+                    out=t[:].bitcast(F32)[:, BANK * g : BANK * (g + 1)].rearrange("p (r u) -> p r u", u=2),
                     in_=turned["dens", i, g][:].rearrange("p (u r) -> p r u", u=2),
                 )
             dens_grouped[i] = t
 
         def dens_quantize(i):
-            codes = ring("dens_codes", [P, 2 * RAYS], U32, 2)
-            scales = ring("dens_scales", [P, 2 * RAYS], U8, 2)
-            quantize(codes[:], scales[:], dens_grouped[i][:])
-            dens_mx[i] = (codes, scales)
+            dens_mx[i] = quantize_chunk("dens", dens_grouped[i][:])
 
         def depth_and_exp(i, s):
             t = ring("trans", [P, 2, 2 * RAYS], F32, 4)
-            d_codes, d_scales = dens_mx[i]
             for u in range(2):
                 acc = bank("mm")
                 for e in range(2):
                     cols = slice(P * (2 * u + e), P * (2 * u + e + 1))
                     for g in range(2):
-                        l_codes, l_scales = len_mx[s, g]
                         rays = slice(RAYS * g, RAYS * (g + 1))
-                        nc.tensor.matmul_mx(
-                            out=acc[:, RAYS * e : RAYS * (e + 1)],
-                            lhsT=l_codes[:, cols].bitcast(FP8X4),
-                            lhsT_scale=l_scales[:, cols],
-                            rhs=d_codes[:, rays].bitcast(FP8X4),
-                            rhs_scale=d_scales[:, rays],
-                            start=(g == 0),
-                            stop=(g == 1),
-                        )
+                        mx_pass(acc[:, RAYS * e : RAYS * (e + 1)], len_mx[s, g], cols, dens_mx[i], rays, g)
                 nc.scalar.activation(
                     out=t[:, u, :].rearrange("p (r e) -> p r e", e=2),
                     in_=acc[:].rearrange("p (e r) -> p r e", e=2),
@@ -236,95 +240,52 @@ def tile_ray_depth_moments_s12_kernel(
                 )
             trans[i, s] = t
 
+        def opac_values(i, s):
+            return turned["opac", i, s][:].bitcast(BF16).rearrange("p (u r e) -> p r u e", u=2, e=2)
+
         def weigh(i, s):
             if s == 0:
                 weight[i] = ring("weight", [P, 2 * 4 * RAYS], BF16, 2)
             nc.vector.tensor_tensor(
                 out=weight[i][:, 4 * RAYS * s : 4 * RAYS * (s + 1)].rearrange("p (r u e) -> p r u e", u=2, e=2),
                 in0=trans[i, s][:].rearrange("p u (r e) -> p r u e", e=2),
-                in1=turned["opac", i, s][:].bitcast(BF16).rearrange("p (u r e) -> p r u e", u=2, e=2),
+                in1=opac_values(i, s),
                 op=mybir.AluOpType.mult,
             )
 
-        def depth_and_exp_tile(i, s, n):
+        def depth_exp_weigh_tile(i, s, n):
             t = ring("trans", [P, 4 * P], F32, 4)
-            d_codes, d_scales = dens_mx[i]
             acc = bank("mm")
             for slot in range(4):
                 cols = slice(P * slot, P * (slot + 1))
                 for g in range(2):
-                    l_codes, l_scales = len_mx[s, g]
                     rays = slice(RAYS * g + P * n, RAYS * g + P * (n + 1))
-                    nc.tensor.matmul_mx(
-                        out=acc[:, cols],
-                        lhsT=l_codes[:, cols].bitcast(FP8X4),
-                        lhsT_scale=l_scales[:, cols],
-                        rhs=d_codes[:, rays].bitcast(FP8X4),
-                        rhs_scale=d_scales[:, rays],
-                        start=(g == 0),
-                        stop=(g == 1),
-                    )
+                    mx_pass(acc[:, cols], len_mx[s, g], cols, dens_mx[i], rays, g)
             nc.scalar.activation(
                 out=t[:].rearrange("p (r t) -> p r t", t=4),
                 in_=acc[:].rearrange("p (t r) -> p r t", t=4),
                 func=EXP,
                 scale=-1.0,
             )
-            trans[i, s, n] = t
-
-        def weigh_tile(i, s, n):
-            t = ring("weight_tile", [P, 4 * P], BF16, 2)
+            w = ring("weight_tile", [P, 4 * P], BF16, 2)
             nc.vector.tensor_tensor(
-                out=t[:].rearrange("p (r u e) -> p r u e", u=2, e=2),
-                in0=trans[i, s, n][:].rearrange("p (r u e) -> p r u e", u=2, e=2),
-                in1=turned["opac", i, s][:]
-                .bitcast(BF16)
-                .rearrange("p (u r e) -> p r u e", u=2, e=2)[:, P * n : P * (n + 1)],
+                out=w[:].rearrange("p (r u e) -> p r u e", u=2, e=2),
+                in0=t[:].rearrange("p (r u e) -> p r u e", u=2, e=2),
+                in1=opac_values(i, s)[:, P * n : P * (n + 1)],
                 op=mybir.AluOpType.mult,
             )
-            weight[i, s, n] = t
-
-        def quantize_part(name, grouped, width):
-            codes = kept(name + "_codes", [P, width], U32)
-            scales = kept(name + "_scales", [P, width], U8)
-            quantize(codes[:], scales[:], grouped)
-            return codes, scales
-
-        def moments_pass(acc, w_mx, rays, s, cols):
-            f_codes, f_scales = func_mx[s]
-            nc.tensor.matmul_mx(
-                out=acc[:, : C // 2],
-                lhsT=w_mx[0][:, rays].bitcast(FP8X4),
-                lhsT_scale=w_mx[1][:, rays],
-                rhs=f_codes[:, cols].bitcast(FP8X4),
-                rhs_scale=f_scales[:, cols],
-                start=(s == 0),
-                stop=(s == 1),
-            )
+            return w
 
         def weight_quantize(i):
-            codes = ring("weight_codes", [P, 2 * RAYS], U32, 2)
-            scales = ring("weight_scales", [P, 2 * RAYS], U8, 2)
-            quantize(codes[:], scales[:], weight[i][:])
-            weight_mx[i] = (codes, scales)
+            weight_mx[i] = quantize_chunk("weight", weight[i][:])
 
         def moments(i):
-            w_codes, w_scales = weight_mx[i]
             t = ring("result", [P, 2 * C], F32, 4)
             for n in range(2):
                 acc = bank("mm")
                 for s in range(2):
-                    f_codes, f_scales = func_mx[s]
                     rays = slice(RAYS * s + P * n, RAYS * s + P * (n + 1))
-                    nc.tensor.matmul_mx(
-                        out=acc[:],
-                        lhsT=w_codes[:, rays].bitcast(FP8X4),
-                        lhsT_scale=w_scales[:, rays],
-                        rhs=f_codes[:].bitcast(FP8X4),
-                        rhs_scale=f_scales[:],
-                        start=(s == 0),
-                        stop=(s == 1),
-                    )
+                    mx_pass(acc[:], weight_mx[i], rays, func_mx[s], slice(0, C), s)
                 nc.scalar.copy(out=t[:, C * n : C * (n + 1)], in_=acc[:])
             nc.sync.dma_start(
                 out=out[RAYS * i : RAYS * (i + 1), :].rearrange("(p n) c -> p (n c)", n=2), in_=t[:]
@@ -341,25 +302,24 @@ def tile_ray_depth_moments_s12_kernel(
         length_interleave(0, 1)
         length_interleave(1, 0)
         length_quantize(0, 1)
-        sort_words("dens", 1)
         length_interleave(1, 1)
         length_quantize(1, 0)
         length_quantize(1, 1)
         depth_and_exp(0, 0)
         turn_rows("dens", 1)
         dens_copy(1)
-        func_turn(0, (nc.scalar.copy, nc.scalar.copy))
-        weigh(0, 0)
-        dens_quantize(1)
+        func_turn(0)
         sort_words("dens", 2)
         sort_words("opac", 1)
+        weigh(0, 0)
+        dens_quantize(1)
+        sort_words("opac", 2)
         depth_and_exp(0, 1)
-        func_turn(1, (nc.scalar.copy, nc.scalar.copy))
+        func_turn(1)
         func_quantize(0)
         weigh(0, 1)
         func_quantize(1)
         weight_quantize(0)
-
 
         last = CHUNKS - 1
         for i in range(1, last):
@@ -381,23 +341,21 @@ def tile_ray_depth_moments_s12_kernel(
         depth_and_exp(last, 0)
         turn_rows("opac", last)
         weigh(last, 0)
-        near = quantize_part("near", weight[last][:, : 4 * RAYS], RAYS)
-        for n in range(2):
-            depth_and_exp_tile(last, 1, n)
-            weigh_tile(last, 1, n)
-        far = [quantize_part("far%d" % n, weight[last, 1, n][:], P) for n in range(2)]
+        near = quantize_kept("near", weight[last][:, : 4 * RAYS], RAYS)
+        far_weight = [depth_exp_weigh_tile(last, 1, n) for n in range(2)]
+        far = [quantize_kept("far%d" % n, far_weight[n][:], P) for n in range(2)]
         moments(last - 1)
         halves = [slice(0, C // 2), slice(C // 2, C)]
-        accs = [[bank("dens"), bank("dens")], [bank("mm"), bank("mm")]]
+        accs = [[bank(tag)[:, : C // 2] for h in range(2)] for tag in ("dens", "mm")]
         for n in range(2):
             for h in range(2):
-                moments_pass(accs[n][h], near, slice(P * n, P * (n + 1)), 0, halves[h])
+                mx_pass(accs[n][h], near, slice(P * n, P * (n + 1)), func_mx[0], halves[h], 0)
         for n in range(2):
             for h in range(2):
-                moments_pass(accs[n][h], far[n], slice(0, P), 1, halves[h])
+                mx_pass(accs[n][h], far[n], slice(0, P), func_mx[1], halves[h], 1)
         rows = out[RAYS * last :, :].rearrange("(p n) c -> p n c", n=2)
         for n in range(2):
             t = ring("result", [P, C], F32, 4)
-            nc.scalar.copy(out=t[:, halves[0]], in_=accs[n][0][:, : C // 2])
-            nc.vector.tensor_copy(out=t[:, halves[1]], in_=accs[n][1][:, : C // 2])
+            nc.scalar.copy(out=t[:, halves[0]], in_=accs[n][0])
+            nc.vector.tensor_copy(out=t[:, halves[1]], in_=accs[n][1])
             nc.sync.dma_start(out=rows[:, n, :], in_=t[:])

from contextlib import ExitStack

import concourse.mybir as mybir
from concourse.masks import make_identity

R, L, H, C = 2048, 1024, 1024, 512
FLOPS = 2 * R * L * L + 2 * H * L * C + 2 * R * L * C

F32 = mybir.dt.float32
BF16 = mybir.dt.bfloat16
I32 = mybir.dt.int32
U32 = mybir.dt.uint32
U8 = mybir.dt.uint8
FP8X4 = mybir.dt.float8_e4m3fn_x4
FP4X4 = mybir.dt.float4_e2m1fn_x4
EXP = mybir.ActivationFunctionType.Exp

P = 128
KP = 512
WORDS = KP // 2
BANK = 512
RAYS = 256
CHUNKS = R // RAYS
BANKS = {"mm": 4, "dens": 2, "opac": 2}


def tile_ray_depth_moments_s12_kernel(
    tc, dens, length, opac, basis_words, basis_scales, mix_words, mix_scales, out
):
    nc = tc.nc
    with ExitStack() as ctx:
        keep = ctx.enter_context(tc.tile_pool(name="keep", bufs=1))
        work = ctx.enter_context(tc.tile_pool(name="work", bufs=2))
        psum = ctx.enter_context(tc.psum_pool(name="psum", bufs=4))
        ctx.enter_context(tc.manual_schedule())

        def kept(name, shape, dtype):
            return keep.tile(shape, dtype, name=name, align_bytes=64)

        def ring(tag, shape, dtype, bufs):
            return work.tile(shape, dtype, name=tag, tag=tag, bufs=bufs, align_bytes=64)

        def bank(tag):
            return psum.tile([P, BANK], F32, name=tag, tag=tag, bufs=BANKS[tag])

        mix_plane = kept("mix_plane", [P, 2, C], U8)
        basis_plane = kept("basis_plane", [P, 2, L], U8)
        nc.gpsimd.memset(mix_plane[:].rearrange("p g n -> p (g n)").bitcast(I32), 0)
        nc.vector.memset(basis_plane[:].rearrange("p g n -> p (g n)").bitcast(I32), 0)
        ident = kept("ident", [P, P], F32)
        make_identity(nc, ident[:])

        mix = kept("mix", [P, 2, 2 * C], U8)
        basis = {}
        len_raw = {}
        rows_in = {}

        def load_scales(plane, src):
            for q in range(4):
                nc.sync.dma_start(
                    out=plane[32 * q : 32 * q + 4].bitcast(I32),
                    in_=src[:, 4 * q : 4 * q + 4, :].rearrange("g r n -> r g n").bitcast(I32),
                )

        def load_basis(s):
            t = kept("basis%d" % s, [P, 2, 2 * KP], U8)
            nc.sync.dma_start(
                out=t[:].bitcast(I32),
                in_=basis_words[:, :, 2 * KP * s : 2 * KP * (s + 1)].rearrange("g p n -> p g n").bitcast(I32),
            )
            basis[s] = t

        def load_length(s, g):
            t = kept("len_raw%d%d" % (s, g), [P, 4, KP], BF16)
            nc.sync.dma_start(
                out=t[:],
                in_=length[KP * g : KP * (g + 1), KP * s : KP * (s + 1)].rearrange("(p j) n -> p j n", j=4),
            )
            len_raw[s, g] = t

        def load_rows(which, src, i):
            t = kept("%s%d" % (which, i), [P, 2 * L], BF16)
            nc.sync.dma_start(
                out=t[:], in_=src[RAYS * i : RAYS * (i + 1), :].rearrange("(p n) k -> p (n k)", n=2)
            )
            rows_in[which, i] = t

        load_rows("dens", dens, 0)
        load_scales(mix_plane, mix_scales)
        load_length(0, 0)
        load_rows("opac", opac, 0)
        nc.sync.dma_start(out=mix[:].bitcast(I32), in_=mix_words.rearrange("g p n -> p g n").bitcast(I32))
        load_scales(basis_plane, basis_scales)
        load_basis(0)
        load_length(0, 1)
        load_basis(1)
        load_length(1, 0)
        load_rows("dens", dens, 1)
        load_length(1, 1)
        for i in range(2, CHUNKS):
            load_rows("opac", opac, i - 1)
            load_rows("dens", dens, i)
        load_rows("opac", opac, CHUNKS - 1)

        len_grouped = {}
        len_mx = {}
        func_sorted = {}
        func_grouped = {}
        func_mx = {}
        sorted_words = {}
        turned = {}
        dens_grouped = {}
        dens_mx = {}
        trans = {}
        weight = {}
        weight_mx = {}

        def quantize(codes, scales, grouped):
            nc.vector.quantize_mx(out=codes[:].bitcast(FP8X4), scales=scales[:], in_=grouped)
            return codes, scales

        def quantize_kept(name, grouped, width):
            return quantize(kept(name + "_codes", [P, width], U32), kept(name + "_scales", [P, width], U8), grouped)

        def quantize_chunk(name, grouped):
            return quantize(
                ring(name + "_codes", [P, 2 * RAYS], U32, 2), ring(name + "_scales", [P, 2 * RAYS], U8, 2), grouped
            )

        def mx_pass(acc, stationary, s_cols, moving, m_cols, g):
            nc.tensor.matmul_mx(
                out=acc,
                lhsT=stationary[0][:, s_cols].bitcast(FP8X4),
                lhsT_scale=stationary[1][:, s_cols],
                rhs=moving[0][:, m_cols].bitcast(FP8X4),
                rhs_scale=moving[1][:, m_cols],
                start=(g == 0),
                stop=(g == 1),
            )

        def length_interleave(s, g):
            t = ring("len_grouped", [P, 4 * KP], BF16, 3)
            nc.vector.tensor_copy(
                out=t[:].rearrange("p (t a b j) -> p a t b j", t=4, b=2, j=4),
                in_=len_raw[s, g][:].rearrange("p j (a b t) -> p a t b j", b=2, t=4),
            )
            len_grouped[s, g] = t

        def length_quantize(s, g):
            len_mx[s, g] = quantize_kept("len%d%d" % (s, g), len_grouped[s, g][:], KP)

        def func_products(s):
            t = kept("func_sorted%d" % s, [P, 4, KP], BF16)
            for ct in range(4):
                acc = bank("mm")
                for g in range(2):
                    nc.tensor.matmul_mx(
                        out=acc[:],
                        lhsT=mix[:, g, 2 * P * ct : 2 * P * (ct + 1)].bitcast(FP4X4),
                        lhsT_scale=mix_plane[:, g, P * ct : P * (ct + 1)],
                        rhs=basis[s][:, g, :].bitcast(FP4X4),
                        rhs_scale=basis_plane[:, g, KP * s : KP * (s + 1)],
                        start=(g == 0),
                        stop=(g == 1),
                    )
                nc.scalar.copy(
                    out=t[:, ct, :].rearrange("p (u m e) -> p u m e", u=2, e=2),
                    in_=acc[:].rearrange("p (m u e) -> p u m e", u=2, e=2),
                )
            func_sorted[s] = t

        def func_turn(s):
            words = func_sorted[s][:].rearrange("p c n -> p (c n)").bitcast(F32)
            t = kept("func_grouped%d" % s, [P, 4 * C], BF16)
            for half in range(2):
                acc = bank("mm")
                for u in range(2):
                    for c in range(2):
                        w0 = WORDS * (2 * half + c) + P * u
                        o0 = 2 * P * u + P * c
                        nc.tensor.transpose(acc[:, o0 : o0 + P], words[:, w0 : w0 + P], ident[:])
                nc.scalar.copy(
                    out=t[:].bitcast(F32)[:, BANK * half : BANK * (half + 1)].rearrange("p (n u) -> p n u", u=2),
                    in_=acc[:].rearrange("p (u n) -> p n u", u=2),
                )
            func_grouped[s] = t

        def func_quantize(s):
            func_mx[s] = quantize_kept("func%d" % s, func_grouped[s][:], C)

        def sort_words(which, i):
            t = ring(which + "_sorted", [P, 2, 2 * WORDS], F32, 2)
            nc.vector.tensor_copy(
                out=t[:].rearrange("p u (a b) -> p a u b", b=4),
                in_=rows_in[which, i][:].bitcast(F32).rearrange("p (a b u) -> p a u b", b=4, u=2),
            )
            sorted_words[which, i] = t

        def turn_rows(which, i):
            for g in range(2):
                acc = bank(which)
                for u in range(2):
                    for n in range(2):
                        if (which, i) in sorted_words:
                            w0 = WORDS * n + P * g
                            src = sorted_words[which, i][:, u, w0 : w0 + P]
                        else:
                            w0 = 2 * WORDS * n + WORDS * g
                            src = rows_in[which, i][:].bitcast(F32)[:, w0 + u : w0 + WORDS : 2]
                        o0 = RAYS * u + P * n
                        nc.tensor.transpose(acc[:, o0 : o0 + P], src, ident[:])
                turned[which, i, g] = acc

        def dens_copy(i):
            t = ring("dens_grouped", [P, 2 * 4 * RAYS], BF16, 2)
            for g in range(2):
                nc.scalar.copy(
                    out=t[:].bitcast(F32)[:, BANK * g : BANK * (g + 1)].rearrange("p (r u) -> p r u", u=2),
                    in_=turned["dens", i, g][:].rearrange("p (u r) -> p r u", u=2),
                )
            dens_grouped[i] = t

        def dens_quantize(i):
            dens_mx[i] = quantize_chunk("dens", dens_grouped[i][:])

        def depth_and_exp(i, s):
            t = ring("trans", [P, 2, 2 * RAYS], F32, 4)
            for u in range(2):
                acc = bank("mm")
                for e in range(2):
                    cols = slice(P * (2 * u + e), P * (2 * u + e + 1))
                    for g in range(2):
                        rays = slice(RAYS * g, RAYS * (g + 1))
                        mx_pass(acc[:, RAYS * e : RAYS * (e + 1)], len_mx[s, g], cols, dens_mx[i], rays, g)
                nc.scalar.activation(
                    out=t[:, u, :].rearrange("p (r e) -> p r e", e=2),
                    in_=acc[:].rearrange("p (e r) -> p r e", e=2),
                    func=EXP,
                    scale=-1.0,
                )
            trans[i, s] = t

        def opac_values(i, s):
            return turned["opac", i, s][:].bitcast(BF16).rearrange("p (u r e) -> p r u e", u=2, e=2)

        def weigh(i, s):
            if s == 0:
                weight[i] = ring("weight", [P, 2 * 4 * RAYS], BF16, 2)
            nc.vector.tensor_tensor(
                out=weight[i][:, 4 * RAYS * s : 4 * RAYS * (s + 1)].rearrange("p (r u e) -> p r u e", u=2, e=2),
                in0=trans[i, s][:].rearrange("p u (r e) -> p r u e", e=2),
                in1=opac_values(i, s),
                op=mybir.AluOpType.mult,
            )

        def depth_exp_weigh_tile(i, s, n):
            t = ring("trans", [P, 4 * P], F32, 4)
            acc = bank("mm")
            for slot in range(4):
                cols = slice(P * slot, P * (slot + 1))
                for g in range(2):
                    rays = slice(RAYS * g + P * n, RAYS * g + P * (n + 1))
                    mx_pass(acc[:, cols], len_mx[s, g], cols, dens_mx[i], rays, g)
            nc.scalar.activation(
                out=t[:].rearrange("p (r t) -> p r t", t=4),
                in_=acc[:].rearrange("p (t r) -> p r t", t=4),
                func=EXP,
                scale=-1.0,
            )
            w = ring("weight_tile", [P, 4 * P], BF16, 2)
            nc.vector.tensor_tensor(
                out=w[:].rearrange("p (r u e) -> p r u e", u=2, e=2),
                in0=t[:].rearrange("p (r u e) -> p r u e", u=2, e=2),
                in1=opac_values(i, s)[:, P * n : P * (n + 1)],
                op=mybir.AluOpType.mult,
            )
            return w

        def weight_quantize(i):
            weight_mx[i] = quantize_chunk("weight", weight[i][:])

        def moments(i):
            t = ring("result", [P, 2 * C], F32, 4)
            for n in range(2):
                acc = bank("mm")
                for s in range(2):
                    rays = slice(RAYS * s + P * n, RAYS * s + P * (n + 1))
                    mx_pass(acc[:], weight_mx[i], rays, func_mx[s], slice(0, C), s)
                nc.scalar.copy(out=t[:, C * n : C * (n + 1)], in_=acc[:])
            nc.sync.dma_start(
                out=out[RAYS * i : RAYS * (i + 1), :].rearrange("(p n) c -> p (n c)", n=2), in_=t[:]
            )

        turn_rows("dens", 0)
        turn_rows("opac", 0)
        dens_copy(0)
        length_interleave(0, 0)
        dens_quantize(0)
        length_quantize(0, 0)
        func_products(0)
        func_products(1)
        length_interleave(0, 1)
        length_interleave(1, 0)
        length_quantize(0, 1)
        length_interleave(1, 1)
        length_quantize(1, 0)
        length_quantize(1, 1)
        depth_and_exp(0, 0)
        turn_rows("dens", 1)
        dens_copy(1)
        func_turn(0)
        sort_words("dens", 2)
        sort_words("opac", 1)
        weigh(0, 0)
        dens_quantize(1)
        sort_words("opac", 2)
        depth_and_exp(0, 1)
        func_turn(1)
        func_quantize(0)
        weigh(0, 1)
        func_quantize(1)
        weight_quantize(0)

        last = CHUNKS - 1
        for i in range(1, last):
            depth_and_exp(i, 0)
            turn_rows("dens", i + 1)
            turn_rows("opac", i)
            dens_copy(i + 1)
            weigh(i, 0)
            dens_quantize(i + 1)
            if i + 2 < CHUNKS:
                sort_words("dens", i + 2)
            depth_and_exp(i, 1)
            weigh(i, 1)
            if i + 2 < CHUNKS:
                sort_words("opac", i + 2)
            moments(i - 1)
            weight_quantize(i)

        depth_and_exp(last, 0)
        turn_rows("opac", last)
        weigh(last, 0)
        near = quantize_kept("near", weight[last][:, : 4 * RAYS], RAYS)
        far_weight = [depth_exp_weigh_tile(last, 1, n) for n in range(2)]
        far = [quantize_kept("far%d" % n, far_weight[n][:], P) for n in range(2)]
        moments(last - 1)
        halves = [slice(0, C // 2), slice(C // 2, C)]
        accs = [[bank(tag)[:, : C // 2] for h in range(2)] for tag in ("dens", "mm")]
        for n in range(2):
            for h in range(2):
                mx_pass(accs[n][h], near, slice(P * n, P * (n + 1)), func_mx[0], halves[h], 0)
        for n in range(2):
            for h in range(2):
                mx_pass(accs[n][h], far[n], slice(0, P), func_mx[1], halves[h], 1)
        rows = out[RAYS * last :, :].rearrange("(p n) c -> p n c", n=2)
        for n in range(2):
            t = ring("result", [P, C], F32, 4)
            nc.scalar.copy(out=t[:, halves[0]], in_=accs[n][0])
            nc.vector.tensor_copy(out=t[:, halves[1]], in_=accs[n][1])
            nc.sync.dma_start(out=rows[:, n, :], in_=t[:])
